import numpy as np
import ml_dtypes


def mxq(x, axis, fmt="e4m3"):
    dtype, down = {"e4m3": (ml_dtypes.float8_e4m3fn, 7), "e5m2": (ml_dtypes.float8_e5m2, 14)}[fmt]
    v = np.moveaxis(np.asarray(x, np.float32).astype(ml_dtypes.bfloat16).astype(np.float64), axis, -1)
    blocks = v.reshape(v.shape[:-1] + (-1, 32))
    amax = np.abs(blocks).max(-1, keepdims=True)
    byte = np.maximum(np.where(amax > 0, np.frexp(amax)[1] - 1 + 127, 0) - down, 1)
    scale = np.exp2(byte - 127.0)
    codes = (blocks / scale).astype(np.float32).astype(dtype).astype(np.float64)
    return np.moveaxis((codes * scale).reshape(v.shape), -1, axis)


WIDE = False


def mx_kscale(k):
    if not WIDE:
        return np.ones(k)
    levels = np.array([10, -10, 5, -5, 0])
    if k % 512:
        return np.exp2(np.random.permutation(np.resize(levels, k // 32))).repeat(32)
    a = np.empty((k // 512, 16))
    for p in range(k // 512):
        a[p, :8] = np.random.permutation(np.resize(levels, 8))
        for g in range(8):
            far = levels[np.abs(levels - a[p, g]) >= 10]
            a[p, g + 8] = far[np.random.randint(len(far))]
    return np.exp2(a.ravel()).repeat(32)


def f64(x):
    return np.asarray(x).astype(np.float64)


def striped(idx):
    return np.tile(idx.reshape(-1, 16).T, (8, 1)).astype(np.uint16)


def unstriped(offs):
    return offs[:16].T.reshape(-1).astype(np.int64)


def pack_weight(w):
    k, n = w.shape
    w = f64(np.asarray(w, np.float32).astype(ml_dtypes.bfloat16)).reshape(k // 32, 32, n)
    amax = np.abs(w).max(1)
    byte = np.clip(np.where(amax > 0, np.frexp(amax)[1] - 1 + 127 - 7, 1), 1, 254)
    scaled = (w * np.exp2(127.0 - byte)[:, None, :]).reshape(k, n).astype(np.float32)
    words = np.ascontiguousarray(scaled.reshape(k // 512, 128, 4, n).transpose(0, 1, 3, 2)).astype(ml_dtypes.float8_e4m3fn).view(np.uint8)
    return words, np.ascontiguousarray(byte.astype(np.uint8).reshape(k // 512, 16, n))


def unpack_weight(words, scales):
    g, p, n, _ = words.shape
    vals = np.ascontiguousarray(words).view(ml_dtypes.float8_e4m3fn).astype(np.float64) * np.repeat(np.exp2(scales.astype(np.float64) - 127.0), 8, axis=1)[..., None]
    return vals.transpose(0, 1, 3, 2).reshape(g * 512, n)


K, T, S, N, D = 1024, 2048, 512, 128, 2
P = 2 ** 7


def setup_inputs():
    n = np.random.standard_normal
    s = mx_kscale(K)[:, None]
    packed_xT = pack_weight(n((K, T)) * s)
    return {
        "x_words": packed_xT[0],
        "x_scales": packed_xT[1],
        "w1": (n((K, N)) / np.sqrt(K) / s).astype(np.float32),
        "wf": (np.tile(np.random.uniform(0.3, 0.7, (D, 1, S)), (1, P, 1))).astype(np.float32),
        "wb": (np.tile(np.random.uniform(0.3, 0.7, (D, 1, S)), (1, P, 1))).astype(np.float32),
        "offs": striped(np.random.permutation(T)[:S]),
        "fwd1": striped(np.random.permutation(S)),
        "bwd1": striped(np.random.permutation(S)),
        "fwd2": striped(np.random.permutation(S)),
        "bwd2": striped(np.random.permutation(S)),
    }


def reference(x_words, x_scales, w1, wf, wb, offs, fwd1, bwd1, fwd2, bwd2):
    xq = unpack_weight(x_words, x_scales)[:, unstriped(offs)]
    y = mxq(f64(w1), 0, "e4m3").T @ xq
    g0 = y[:, unstriped(fwd1)]
    g1 = y[:, unstriped(fwd2)]
    p1 = g0 * f64(wf)[0, :1] + g1 * f64(wf)[1, :1]
    p0 = p1[:, unstriped(bwd1)] * f64(wb)[0, :1] + p1[:, unstriped(bwd2)] * f64(wb)[1, :1]
    rr = p1 + 0.5 * (y - p0)
    return np.minimum(np.maximum(rr, np.minimum(g0, g1)), np.maximum(g0, g1))

@@ -1,0 +1,125 @@
+from contextlib import ExitStack
+
+import concourse.mybir as mybir
+
+K, T, S, M = 1024, 2048, 512, 128
+FLOPS = 2 * K * S * M
+
+F32 = mybir.dt.float32
+BF16 = mybir.dt.bfloat16
+I32 = mybir.dt.int32
+U32 = mybir.dt.uint32
+U16 = mybir.dt.uint16
+U8 = mybir.dt.uint8
+FP8X4 = mybir.dt.float8_e4m3fn_x4
+ALU = mybir.AluOpType
+COPY = mybir.ActivationFunctionType.Copy
+
+P = 128
+PASSES = K // 512
+HALF = S // 2
+
+
+def tile_picked_ymaccor_clamp_p_kernel(tc, x_words, x_scales, w1, wf, wb, offs, fwd1, bwd1, fwd2, bwd2, out):
+    nc = tc.nc
+    with ExitStack() as ctx:
+        lists = ctx.enter_context(tc.tile_pool(name="lists", bufs=1))
+        sb = ctx.enter_context(tc.tile_pool(name="sb", bufs=1))
+        psum = ctx.enter_context(tc.psum_pool(name="psum", bufs=1))
+
+        def load_list(src, name):
+            t = lists.tile([P, S // 16], U16, name=name)
+            nc.sync.dma_start(t[:], src)
+            return t
+
+        def cols(h):
+            return slice(h * HALF, (h + 1) * HALF)
+
+        def entries(lst, h):
+            return lst[:, h * HALF // 16 : (h + 1) * HALF // 16]
+
+        xs = sb.tile([P, T], U8, name="xs", align_bytes=64)
+        nc.gpsimd.memset(xs[:].bitcast(I32), 0)
+        xw = [sb.tile([P, T], U32, name="xw%d" % g, align_bytes=64) for g in range(PASSES)]
+        w_raw = sb.tile([P, PASSES, 4, M], F32, name="w_raw")
+
+        def load_words(g):
+            nc.sync.dma_start(xw[g][:].bitcast(I32), x_words[g].rearrange("p n t -> p (n t)").bitcast(I32))
+
+        offs_t = load_list(offs, "offs_t")
+        load_words(0)
+        for q in (0, 1):
+            nc.gpsimd.dma_start(xs[32 * q : 32 * q + 8, :].bitcast(I32), x_scales[:, 4 * q : 4 * q + 4, :].bitcast(I32))
+        for q in (2, 3):
+            for g in range(PASSES):
+                nc.scalar.dma_start(xs[32 * q + 4 * g : 32 * q + 4 * g + 4, :].bitcast(I32), x_scales[g, 4 * q : 4 * q + 4, :].bitcast(I32))
+        nc.sync.dma_start(w_raw[:], w1.rearrange("(g p j) m -> p g j m", g=PASSES, j=4))
+        load_words(1)
+        f0 = load_list(fwd1, "f0")
+        f1 = load_list(fwd2, "f1")
+        wf_t = sb.tile([P, 2, S], F32, name="wf_t")
+        nc.sync.dma_start(wf_t[:], wf.rearrange("d p s -> p d s"))
+        b0 = load_list(bwd1, "b0")
+        b1 = load_list(bwd2, "b1")
+        wb_t = sb.tile([P, 2, S], F32, name="wb_t")
+        nc.sync.dma_start(wb_t[:], wb.rearrange("d p s -> p d s"))
+
+        w_bf = sb.tile([P, PASSES, M, 4], BF16, name="w_bf", align_bytes=64)
+        nc.scalar.copy(w_bf[:], w_raw[:].rearrange("p g j m -> p g m j"))
+        w_codes = sb.tile([P, PASSES * M], U32, name="w_codes", align_bytes=64)
+        w_scales = sb.tile([P, PASSES * M], U8, name="w_scales", align_bytes=64)
+
+        gw = [sb.tile([P, S], U32, name="gw%d" % g, align_bytes=64) for g in range(PASSES)]
+        gs = sb.tile([P, S], U8, name="gs", align_bytes=64)
+        nc.vector.tensor_copy(gw[0][:], xw[0][:].indirect(offs_t[:]))
+        nc.vector.tensor_copy(gs[:], xs[:].indirect(offs_t[:]))
+        nc.vector.quantize_mx(out=w_codes[:].bitcast(FP8X4), scales=w_scales[:], in_=w_bf[:].rearrange("p g m j -> p (g m j)"))
+        y = sb.tile([P, S], F32, name="y")
+        acc = [psum.tile([P, HALF], F32, name="acc%d" % h) for h in range(2)]
+
+        def product(h, g):
+            nc.tensor.matmul_mx(
+                out=acc[h][:],
+                lhsT=w_codes[:, g * M : (g + 1) * M].bitcast(FP8X4),
+                lhsT_scale=w_scales[:, g * M : (g + 1) * M],
+                rhs=gw[g][:, cols(h)].bitcast(FP8X4),
+                rhs_scale=gs[4 * g : P, cols(h)],
+                start=(g == 0),
+                stop=(g == PASSES - 1),
+            )
+
+        for h in range(2):
+            product(h, 0)
+        for h in range(2):
+            nc.vector.tensor_copy(gw[1][:, cols(h)], xw[1][:].indirect(entries(offs_t, h)))
+            product(h, 1)
+        nc.scalar.copy(y[:, cols(0)], acc[0][:])
+        nc.vector.tensor_copy(y[:, cols(1)], acc[1][:])
+
+        def ftile(name):
+            return sb.tile([P, S], F32, name=name)
+
+        g0, g1, t0, t1, p1, lo, hi, base, u0, u1, r0, r1, c0, res = [ftile(n) for n in ("g0", "g1", "t0", "t1", "p1", "lo", "hi", "base", "u0", "u1", "r0", "r1", "c0", "res")]
+        A, B = cols(0), cols(1)
+        tt = nc.vector.tensor_tensor
+        nc.vector.tensor_copy(g0[:, A], y[:].indirect(entries(f0, 0)))
+        nc.vector.tensor_copy(g0[:, B], y[:].indirect(entries(f0, 1)))
+        nc.vector.tensor_copy(g1[:, A], y[:].indirect(entries(f1, 0)))
+        nc.vector.tensor_copy(g1[:, B], y[:].indirect(entries(f1, 1)))
+        tt(t0[:], g0[:], wf_t[:, 0, :], ALU.mult)
+        tt(t1[:, A], g1[:, A], wf_t[:, 1, A], ALU.mult)
+        tt(t1[:, B], g1[:, B], wf_t[:, 1, B], ALU.mult)
+        tt(p1[:, A], t0[:, A], t1[:, A], ALU.add)
+        tt(p1[:, B], t0[:, B], t1[:, B], ALU.add)
+        tt(lo[:], g0[:], g1[:], ALU.min)
+        for h in range(2):
+            c = cols(h)
+            tt(u0[:, c], p1[:].indirect(entries(b0, h)), wb_t[:, 0, c], ALU.mult)
+            tt(u1[:, c], p1[:].indirect(entries(b1, h)), wb_t[:, 1, c], ALU.mult)
+            nc.vector.scalar_tensor_tensor(base[:, c], y[:, c], 0.5, p1[:, c], ALU.mult, ALU.add)
+            tt(hi[:, c], g0[:, c], g1[:, c], ALU.max)
+            nc.vector.scalar_tensor_tensor(r0[:, c], u0[:, c], -0.5, base[:, c], ALU.mult, ALU.add)
+            nc.vector.scalar_tensor_tensor(r1[:, c], u1[:, c], -0.5, r0[:, c], ALU.mult, ALU.add)
+            tt(c0[:, c], r1[:, c], lo[:, c], ALU.max)
+            tt(res[:, c], c0[:, c], hi[:, c], ALU.min)
+            nc.sync.dma_start(out[:, c], res[:, c])

@@ -1,6 +1,7 @@
 from contextlib import ExitStack
 
 import concourse.mybir as mybir
+from concourse.masks import make_identity
 
 K, T, S, M = 1024, 2048, 512, 128
 FLOPS = 2 * K * S * M
@@ -19,6 +20,10 @@ P = 128
 PASSES = K // 512
 HALF = S // 2
 
+BLK = 128
+CHUNKS1 = [(0, 2, True), (2, 1, True), (3, 1, False)]
+CHUNKS2 = [(0, 2, True), (2, 1, True), (3, 1, False)]
+
 
 def tile_picked_ymaccor_clamp_p_kernel(tc, x_words, x_scales, w1, wf, wb, offs, fwd1, bwd1, fwd2, bwd2, out):
     nc = tc.nc
@@ -32,14 +37,18 @@ def tile_picked_ymaccor_clamp_p_kernel(tc, x_words, x_scales, w1, wf, wb, offs, 
             nc.sync.dma_start(t[:], src)
             return t
 
-        def cols(h):
-            return slice(h * HALF, (h + 1) * HALF)
+        def cols(first, n):
+            return slice(first * BLK, (first + n) * BLK)
 
-        def entries(lst, h):
-            return lst[:, h * HALF // 16 : (h + 1) * HALF // 16]
+        def entries(lst, first, n):
+            return lst[:, first * BLK // 16 : (first + n) * BLK // 16]
 
         xs = sb.tile([P, T], U8, name="xs", align_bytes=64)
         nc.gpsimd.memset(xs[:].bitcast(I32), 0)
+        wrow = sb.tile([P, P], F32, name="wrow")
+        nc.gpsimd.memset(wrow[:], 0.0)
+        ident = sb.tile([P, P], F32, name="ident")
+        make_identity(nc, ident[:])
         xw = [sb.tile([P, T], U32, name="xw%d" % g, align_bytes=64) for g in range(PASSES)]
         w_raw = sb.tile([P, PASSES, 4, M], F32, name="w_raw")
 
@@ -47,22 +56,29 @@ def tile_picked_ymaccor_clamp_p_kernel(tc, x_words, x_scales, w1, wf, wb, offs, 
             nc.sync.dma_start(xw[g][:].bitcast(I32), x_words[g].rearrange("p n t -> p (n t)").bitcast(I32))
 
         offs_t = load_list(offs, "offs_t")
-        load_words(0)
-        for q in (0, 1):
-            nc.gpsimd.dma_start(xs[32 * q : 32 * q + 8, :].bitcast(I32), x_scales[:, 4 * q : 4 * q + 4, :].bitcast(I32))
-        for q in (2, 3):
-            for g in range(PASSES):
-                nc.scalar.dma_start(xs[32 * q + 4 * g : 32 * q + 4 * g + 4, :].bitcast(I32), x_scales[g, 4 * q : 4 * q + 4, :].bitcast(I32))
         nc.sync.dma_start(w_raw[:], w1.rearrange("(g p j) m -> p g j m", g=PASSES, j=4))
+
+        def load_scales(q):
+            for g in range(PASSES):
+                nc.sync.dma_start(xs[32 * q + 4 * g : 32 * q + 4 * g + 4, :].bitcast(I32), x_scales[g, 4 * q : 4 * q + 4, :].bitcast(I32))
+
+        load_scales(0)
+        load_words(0)
+        for q in range(1, 4):
+            load_scales(q)
         load_words(1)
-        f0 = load_list(fwd1, "f0")
-        f1 = load_list(fwd2, "f1")
-        wf_t = sb.tile([P, 2, S], F32, name="wf_t")
-        nc.sync.dma_start(wf_t[:], wf.rearrange("d p s -> p d s"))
-        b0 = load_list(bwd1, "b0")
-        b1 = load_list(bwd2, "b1")
-        wb_t = sb.tile([P, 2, S], F32, name="wb_t")
-        nc.sync.dma_start(wb_t[:], wb.rearrange("d p s -> p d s"))
+        nc.gpsimd.dma_start(wrow[0:8, :], wf[:, 0, :].rearrange("d (c p) -> d c p", p=BLK))
+        nc.gpsimd.dma_start(wrow[8:16, :], wb[:, 0, :].rearrange("d (c p) -> d c p", p=BLK))
+        f = [load_list(fwd1, "f0"), load_list(fwd2, "f1")]
+        v1 = min([c[0] for c in CHUNKS1 if not c[2]] + [4])
+        v2 = min([c[0] for c in CHUNKS2 if not c[2]] + [4])
+        if v1 < 4:
+            wf_t = sb.tile([P, 2, S - v1 * BLK], F32, name="wf_t")
+            nc.sync.dma_start(wf_t[:], wf[:, :, v1 * BLK :].rearrange("d p s -> p d s"))
+        b = [load_list(bwd1, "b0"), load_list(bwd2, "b1")]
+        if v2 < 4:
+            wb_t = sb.tile([P, 2, S - v2 * BLK], F32, name="wb_t")
+            nc.sync.dma_start(wb_t[:], wb[:, :, v2 * BLK :].rearrange("d p s -> p d s"))
 
         w_bf = sb.tile([P, PASSES, M, 4], BF16, name="w_bf", align_bytes=64)
         nc.scalar.copy(w_bf[:], w_raw[:].rearrange("p g j m -> p g m j"))
@@ -71,55 +87,101 @@ def tile_picked_ymaccor_clamp_p_kernel(tc, x_words, x_scales, w1, wf, wb, offs, 
 
         gw = [sb.tile([P, S], U32, name="gw%d" % g, align_bytes=64) for g in range(PASSES)]
         gs = sb.tile([P, S], U8, name="gs", align_bytes=64)
+        nc.vector.quantize_mx(out=w_codes[:].bitcast(FP8X4), scales=w_scales[:], in_=w_bf[:].rearrange("p g m j -> p (g m j)"))
         nc.vector.tensor_copy(gw[0][:], xw[0][:].indirect(offs_t[:]))
         nc.vector.tensor_copy(gs[:], xs[:].indirect(offs_t[:]))
-        nc.vector.quantize_mx(out=w_codes[:].bitcast(FP8X4), scales=w_scales[:], in_=w_bf[:].rearrange("p g m j -> p (g m j)"))
         y = sb.tile([P, S], F32, name="y")
-        acc = [psum.tile([P, HALF], F32, name="acc%d" % h) for h in range(2)]
+        acc = [psum.tile([P, HALF], F32, name="acc%d" % h, tag="sum%d" % h) for h in range(2)]
 
         def product(h, g):
             nc.tensor.matmul_mx(
                 out=acc[h][:],
                 lhsT=w_codes[:, g * M : (g + 1) * M].bitcast(FP8X4),
                 lhsT_scale=w_scales[:, g * M : (g + 1) * M],
-                rhs=gw[g][:, cols(h)].bitcast(FP8X4),
-                rhs_scale=gs[4 * g : P, cols(h)],
+                rhs=gw[g][:, cols(2 * h, 2)].bitcast(FP8X4),
+                rhs_scale=gs[4 * g : P, cols(2 * h, 2)],
                 start=(g == 0),
                 stop=(g == PASSES - 1),
             )
 
         for h in range(2):
             product(h, 0)
+
+        wt_ps = psum.tile([P, BLK], F32, name="wt_ps", tag="turn", bufs=6)
+        nc.tensor.transpose(wt_ps[:], wrow[:], ident[:])
+        wcol = sb.tile([P, 16], F32, name="wcol")
+        nc.scalar.copy(wcol[:, 0:8], wt_ps[:, 0:8])
+        nc.scalar.activation(wcol[:, 8:16], wt_ps[:, 8:16], COPY, scale=-0.5)
+
         for h in range(2):
-            nc.vector.tensor_copy(gw[1][:, cols(h)], xw[1][:].indirect(entries(offs_t, h)))
+            nc.vector.tensor_copy(gw[1][:, cols(2 * h, 2)], xw[1][:].indirect(entries(offs_t, 2 * h, 2)))
             product(h, 1)
-        nc.scalar.copy(y[:, cols(0)], acc[0][:])
-        nc.vector.tensor_copy(y[:, cols(1)], acc[1][:])
+        nc.scalar.copy(y[:, cols(0, 2)], acc[0][:])
+        nc.vector.tensor_copy(y[:, cols(2, 2)], acc[1][:])
 
         def ftile(name):
             return sb.tile([P, S], F32, name=name)
 
-        g0, g1, t0, t1, p1, lo, hi, base, u0, u1, r0, r1, c0, res = [ftile(n) for n in ("g0", "g1", "t0", "t1", "p1", "lo", "hi", "base", "u0", "u1", "r0", "r1", "c0", "res")]
-        A, B = cols(0), cols(1)
+        g = [ftile("g0"), ftile("g1")]
+        t = [ftile("t0"), ftile("t1")]
+        u = [ftile("u0"), ftile("u1")]
+        tT = [ftile("tT0"), ftile("tT1")]
+        uT = [ftile("uT0"), ftile("uT1")]
+        p1, lo, hi, base, r0, r1, c0, res, hyT = [ftile(n) for n in ("p1", "lo", "hi", "base", "r0", "r1", "c0", "res", "hyT")]
         tt = nc.vector.tensor_tensor
-        nc.vector.tensor_copy(g0[:, A], y[:].indirect(entries(f0, 0)))
-        nc.vector.tensor_copy(g0[:, B], y[:].indirect(entries(f0, 1)))
-        nc.vector.tensor_copy(g1[:, A], y[:].indirect(entries(f1, 0)))
-        nc.vector.tensor_copy(g1[:, B], y[:].indirect(entries(f1, 1)))
-        tt(t0[:], g0[:], wf_t[:, 0, :], ALU.mult)
-        tt(t1[:, A], g1[:, A], wf_t[:, 1, A], ALU.mult)
-        tt(t1[:, B], g1[:, B], wf_t[:, 1, B], ALU.mult)
-        tt(p1[:, A], t0[:, A], t1[:, A], ALU.add)
-        tt(p1[:, B], t0[:, B], t1[:, B], ALU.add)
-        tt(lo[:], g0[:], g1[:], ALU.min)
-        for h in range(2):
-            c = cols(h)
-            tt(u0[:, c], p1[:].indirect(entries(b0, h)), wb_t[:, 0, c], ALU.mult)
-            tt(u1[:, c], p1[:].indirect(entries(b1, h)), wb_t[:, 1, c], ALU.mult)
-            nc.vector.scalar_tensor_tensor(base[:, c], y[:, c], 0.5, p1[:, c], ALU.mult, ALU.add)
-            tt(hi[:, c], g0[:, c], g1[:, c], ALU.max)
-            nc.vector.scalar_tensor_tensor(r0[:, c], u0[:, c], -0.5, base[:, c], ALU.mult, ALU.add)
-            nc.vector.scalar_tensor_tensor(r1[:, c], u1[:, c], -0.5, r0[:, c], ALU.mult, ALU.add)
-            tt(c0[:, c], r1[:, c], lo[:, c], ALU.max)
-            tt(res[:, c], c0[:, c], hi[:, c], ALU.min)
-            nc.sync.dma_start(out[:, c], res[:, c])
+        stt = nc.vector.scalar_tensor_tensor
+
+        def turn_scaled(dst, src, first, n, col):
+            for i in range(first, first + n):
+                ps = psum.tile([P, BLK], F32, name="turn_ps", tag="turn", bufs=6)
+                nc.tensor.transpose(ps[:], src[:, cols(i, 1)], ident[:])
+                nc.scalar.activation(dst[:, cols(i, 1)], ps[:], COPY, scale=(0.5 if col is None else wcol[:, col + i : col + i + 1]))
+
+        def add_back(ps, src, first, n, start, stop):
+            for i in range(n):
+                nc.tensor.matmul(ps[:, cols(i, 1)], src[:, cols(first + i, 1)], ident[:], start=(start and i == 0), stop=(stop and i == n - 1), is_transpose=True)
+
+        A, B = cols(0, 2), cols(2, 2)
+        c2, c3 = cols(2, 1), cols(3, 1)
+        turned = ((0, 2), (2, 1))
+        for j, (first, n) in enumerate(turned):
+            turn_scaled(hyT, y, first, n, None)
+        for j, (first, n) in enumerate(turned):
+            for d in range(2):
+                nc.vector.tensor_copy(g[d][:, cols(first, n)], y[:].indirect(entries(f[d], first, n)))
+                turn_scaled(tT[d], g[d], first, n, 4 * d)
+            p1_ps = psum.tile([P, n * BLK], F32, name="p1_ps%d" % j, tag="sum%d" % j)
+            for d in range(2):
+                add_back(p1_ps, tT[d], first, n, d == 0, d == 1)
+            nc.scalar.copy(p1[:, cols(first, n)], p1_ps[:])
+        for d in range(2):
+            nc.vector.tensor_copy(g[d][:, c3], y[:].indirect(entries(f[d], 3, 1)))
+        for d in range(2):
+            tt(t[d][:, c3], g[d][:, c3], wf_t[:, d, :], ALU.mult)
+        tt(lo[:], g[0][:], g[1][:], ALU.min)
+        tt(p1[:, c3], t[0][:, c3], t[1][:, c3], ALU.add)
+        tt(hi[:], g[0][:], g[1][:], ALU.max)
+        rr = [psum.tile([P, n * BLK], F32, name="rr%d" % j, tag="sum%d" % j) for j, (first, n) in enumerate(turned)]
+        for j, (first, n) in enumerate(turned):
+            add_back(rr[j], hyT, first, n, True, False)
+            for d in range(2):
+                add_back(rr[j], tT[d], first, n, False, False)
+
+        for j, (first, n) in enumerate(turned):
+            for d in range(2):
+                nc.vector.tensor_copy(u[d][:, cols(first, n)], p1[:].indirect(entries(b[d], first, n)))
+                turn_scaled(uT[d], u[d], first, n, 8 + 4 * d)
+            for d in range(2):
+                add_back(rr[j], uT[d], first, n, False, d == 1)
+        for d in range(2):
+            tt(u[d][:, c3], p1[:].indirect(entries(b[d], 3, 1)), wb_t[:, d, :], ALU.mult)
+        stt(base[:, c3], y[:, c3], 0.5, p1[:, c3], ALU.mult, ALU.add)
+        stt(r0[:, c3], u[0][:, c3], -0.5, base[:, c3], ALU.mult, ALU.add)
+        stt(r1[:, c3], u[1][:, c3], -0.5, r0[:, c3], ALU.mult, ALU.add)
+        tt(c0[:, c3], r1[:, c3], lo[:, c3], ALU.max)
+        tt(c0[:, A], rr[0][:], lo[:, A], ALU.max)
+        tt(c0[:, c2], rr[1][:], lo[:, c2], ALU.max)
+        tt(res[:, A], c0[:, A], hi[:, A], ALU.min)
+        nc.sync.dma_start(out[:, A], res[:, A])
+        tt(res[:, B], c0[:, B], hi[:, B], ALU.min)
+        nc.sync.dma_start(out[:, B], res[:, B])

@@ -17,12 +17,15 @@ ALU = mybir.AluOpType
 COPY = mybir.ActivationFunctionType.Copy
 
 P = 128
-PASSES = K // 512
-HALF = S // 2
-
+PACK = 4
+PASSES = K // (P * PACK)
+QUADRANTS = P // 32
 BLK = 128
-CHUNKS1 = [(0, 2, True), (2, 1, True), (3, 1, False)]
-CHUNKS2 = [(0, 2, True), (2, 1, True), (3, 1, False)]
+BLOCKS = S // BLK
+TURNED = BLOCKS - 1
+LAST = TURNED
+SUM_BANKS = 2
+TURN_BANKS = 8 - SUM_BANKS
 
 
 def tile_picked_ymaccor_clamp_p_kernel(tc, x_words, x_scales, w1, wf, wb, offs, fwd1, bwd1, fwd2, bwd2, out):
@@ -32,74 +35,82 @@ def tile_picked_ymaccor_clamp_p_kernel(tc, x_words, x_scales, w1, wf, wb, offs, 
         sb = ctx.enter_context(tc.tile_pool(name="sb", bufs=1))
         psum = ctx.enter_context(tc.psum_pool(name="psum", bufs=1))
 
-        def load_list(src, name):
-            t = lists.tile([P, S // 16], U16, name=name)
-            nc.sync.dma_start(t[:], src)
-            return t
-
-        def cols(first, n):
+        def cols(first, n=1):
             return slice(first * BLK, (first + n) * BLK)
 
         def entries(lst, first, n):
             return lst[:, first * BLK // 16 : (first + n) * BLK // 16]
 
-        xs = sb.tile([P, T], U8, name="xs", align_bytes=64)
-        nc.gpsimd.memset(xs[:].bitcast(I32), 0)
-        wrow = sb.tile([P, P], F32, name="wrow")
-        nc.gpsimd.memset(wrow[:], 0.0)
-        ident = sb.tile([P, P], F32, name="ident")
+        def load_list(src, name):
+            lst = lists.tile([P, S // 16], U16, name=name)
+            nc.sync.dma_start(lst[:], src)
+            return lst
+
+        def field(name, width=S):
+            return sb.tile([P, width], F32, name=name)
+
+        def sum_bank(bank, n, name):
+            return psum.tile([P, n * BLK], F32, name=name, tag="sum%d" % bank)
+
+        def turn_bank():
+            return psum.tile([P, BLK], F32, name="turn", tag="turn", bufs=TURN_BANKS)
+
+        x_scale_table = sb.tile([P, T], U8, name="x_scale_table", align_bytes=64)
+        nc.gpsimd.memset(x_scale_table[:].bitcast(I32), 0)
+        weight_rows = field("weight_rows", BLK)
+        nc.gpsimd.memset(weight_rows[:], 0.0)
+        ident = field("ident", P)
         make_identity(nc, ident[:])
-        xw = [sb.tile([P, T], U32, name="xw%d" % g, align_bytes=64) for g in range(PASSES)]
-        w_raw = sb.tile([P, PASSES, 4, M], F32, name="w_raw")
+
+        x_word_table = [sb.tile([P, T], U32, name="x_word_table%d" % g, align_bytes=64) for g in range(PASSES)]
+        w_raw = sb.tile([P, PASSES, PACK, M], F32, name="w_raw")
 
         def load_words(g):
-            nc.sync.dma_start(xw[g][:].bitcast(I32), x_words[g].rearrange("p n t -> p (n t)").bitcast(I32))
-
-        offs_t = load_list(offs, "offs_t")
-        nc.sync.dma_start(w_raw[:], w1.rearrange("(g p j) m -> p g j m", g=PASSES, j=4))
+            nc.sync.dma_start(x_word_table[g][:].bitcast(I32), x_words[g].rearrange("p n t -> p (n t)").bitcast(I32))
 
         def load_scales(q):
             for g in range(PASSES):
-                nc.sync.dma_start(xs[32 * q + 4 * g : 32 * q + 4 * g + 4, :].bitcast(I32), x_scales[g, 4 * q : 4 * q + 4, :].bitcast(I32))
+                row = 32 * q + 4 * g
+                nc.sync.dma_start(x_scale_table[row : row + 4, :].bitcast(I32), x_scales[g, 4 * q : 4 * q + 4, :].bitcast(I32))
 
+        idx = load_list(offs, "idx")
+        nc.sync.dma_start(w_raw[:], w1.rearrange("(g p t) m -> p g t m", g=PASSES, t=PACK))
         load_scales(0)
         load_words(0)
-        for q in range(1, 4):
+        for q in range(1, QUADRANTS):
             load_scales(q)
         load_words(1)
-        nc.gpsimd.dma_start(wrow[0:8, :], wf[:, 0, :].rearrange("d (c p) -> d c p", p=BLK))
-        nc.gpsimd.dma_start(wrow[8:16, :], wb[:, 0, :].rearrange("d (c p) -> d c p", p=BLK))
-        f = [load_list(fwd1, "f0"), load_list(fwd2, "f1")]
-        v1 = min([c[0] for c in CHUNKS1 if not c[2]] + [4])
-        v2 = min([c[0] for c in CHUNKS2 if not c[2]] + [4])
-        if v1 < 4:
-            wf_t = sb.tile([P, 2, S - v1 * BLK], F32, name="wf_t")
-            nc.sync.dma_start(wf_t[:], wf[:, :, v1 * BLK :].rearrange("d p s -> p d s"))
-        b = [load_list(bwd1, "b0"), load_list(bwd2, "b1")]
-        if v2 < 4:
-            wb_t = sb.tile([P, 2, S - v2 * BLK], F32, name="wb_t")
-            nc.sync.dma_start(wb_t[:], wb[:, :, v2 * BLK :].rearrange("d p s -> p d s"))
+        for s, weights in enumerate((wf, wb)):
+            rows = weight_rows[2 * TURNED * s : 2 * TURNED * (s + 1), :]
+            nc.gpsimd.dma_start(rows, weights[:, 0, cols(0, TURNED)].rearrange("d (b c) -> d b c", c=BLK))
+        fwd = [load_list(fwd1, "f0"), load_list(fwd2, "f1")]
+        wf_last = sb.tile([P, 2, BLK], F32, name="wf_last")
+        nc.sync.dma_start(wf_last[:], wf[:, :, cols(LAST)].rearrange("d p c -> p d c"))
+        bwd = [load_list(bwd1, "b0"), load_list(bwd2, "b1")]
+        wb_last = sb.tile([P, 2, BLK], F32, name="wb_last")
+        nc.sync.dma_start(wb_last[:], wb[:, :, cols(LAST)].rearrange("d p c -> p d c"))
 
-        w_bf = sb.tile([P, PASSES, M, 4], BF16, name="w_bf", align_bytes=64)
-        nc.scalar.copy(w_bf[:], w_raw[:].rearrange("p g j m -> p g m j"))
+        w_bf = sb.tile([P, PASSES, M, PACK], BF16, name="w_bf", align_bytes=64)
+        nc.scalar.copy(w_bf[:], w_raw[:].rearrange("p g t m -> p g m t"))
         w_codes = sb.tile([P, PASSES * M], U32, name="w_codes", align_bytes=64)
         w_scales = sb.tile([P, PASSES * M], U8, name="w_scales", align_bytes=64)
+        nc.vector.quantize_mx(out=w_codes[:].bitcast(FP8X4), scales=w_scales[:], in_=w_bf[:].rearrange("p g m t -> p (g m t)"))
 
-        gw = [sb.tile([P, S], U32, name="gw%d" % g, align_bytes=64) for g in range(PASSES)]
-        gs = sb.tile([P, S], U8, name="gs", align_bytes=64)
-        nc.vector.quantize_mx(out=w_codes[:].bitcast(FP8X4), scales=w_scales[:], in_=w_bf[:].rearrange("p g m j -> p (g m j)"))
-        nc.vector.tensor_copy(gw[0][:], xw[0][:].indirect(offs_t[:]))
-        nc.vector.tensor_copy(gs[:], xs[:].indirect(offs_t[:]))
-        y = sb.tile([P, S], F32, name="y")
-        acc = [psum.tile([P, HALF], F32, name="acc%d" % h, tag="sum%d" % h) for h in range(2)]
+        x_codes = [sb.tile([P, S], U32, name="x_codes%d" % g, align_bytes=64) for g in range(PASSES)]
+        x_scale = sb.tile([P, S], U8, name="x_scale", align_bytes=64)
+        nc.vector.tensor_copy(x_codes[0][:], x_word_table[0][:].indirect(idx[:]))
+        nc.vector.tensor_copy(x_scale[:], x_scale_table[:].indirect(idx[:]))
+
+        y_ps = [sum_bank(h, 2, "y_ps%d" % h) for h in range(2)]
 
         def product(h, g):
+            c = cols(2 * h, 2)
             nc.tensor.matmul_mx(
-                out=acc[h][:],
+                out=y_ps[h][:],
                 lhsT=w_codes[:, g * M : (g + 1) * M].bitcast(FP8X4),
                 lhsT_scale=w_scales[:, g * M : (g + 1) * M],
-                rhs=gw[g][:, cols(2 * h, 2)].bitcast(FP8X4),
-                rhs_scale=gs[4 * g : P, cols(2 * h, 2)],
+                rhs=x_codes[g][:, c].bitcast(FP8X4),
+                rhs_scale=x_scale[4 * g : P, c],
                 start=(g == 0),
                 stop=(g == PASSES - 1),
             )
@@ -107,81 +118,93 @@ def tile_picked_ymaccor_clamp_p_kernel(tc, x_words, x_scales, w1, wf, wb, offs, 
         for h in range(2):
             product(h, 0)
 
-        wt_ps = psum.tile([P, BLK], F32, name="wt_ps", tag="turn", bufs=6)
-        nc.tensor.transpose(wt_ps[:], wrow[:], ident[:])
-        wcol = sb.tile([P, 16], F32, name="wcol")
-        nc.scalar.copy(wcol[:, 0:8], wt_ps[:, 0:8])
-        nc.scalar.activation(wcol[:, 8:16], wt_ps[:, 8:16], COPY, scale=-0.5)
+        weight_ps = turn_bank()
+        nc.tensor.transpose(weight_ps[:], weight_rows[:], ident[:])
+        wf_cols = field("wf_cols", 2 * TURNED)
+        wb_cols = field("wb_cols", 2 * TURNED)
+        nc.scalar.copy(wf_cols[:], weight_ps[:, 0 : 2 * TURNED])
+        nc.scalar.activation(wb_cols[:], weight_ps[:, 2 * TURNED : 4 * TURNED], COPY, scale=-0.5)
 
         for h in range(2):
-            nc.vector.tensor_copy(gw[1][:, cols(2 * h, 2)], xw[1][:].indirect(entries(offs_t, 2 * h, 2)))
+            nc.vector.tensor_copy(x_codes[1][:, cols(2 * h, 2)], x_word_table[1][:].indirect(entries(idx, 2 * h, 2)))
             product(h, 1)
-        nc.scalar.copy(y[:, cols(0, 2)], acc[0][:])
-        nc.vector.tensor_copy(y[:, cols(2, 2)], acc[1][:])
+        y = field("y")
+        nc.scalar.copy(y[:, cols(0, 2)], y_ps[0][:])
+        nc.vector.tensor_copy(y[:, cols(2, 2)], y_ps[1][:])
 
-        def ftile(name):
-            return sb.tile([P, S], F32, name=name)
+        def gather(dst, window, lst, first, n):
+            nc.vector.tensor_copy(dst[:, cols(first, n)], window[:].indirect(entries(lst, first, n)))
 
-        g = [ftile("g0"), ftile("g1")]
-        t = [ftile("t0"), ftile("t1")]
-        u = [ftile("u0"), ftile("u1")]
-        tT = [ftile("tT0"), ftile("tT1")]
-        uT = [ftile("uT0"), ftile("uT1")]
-        p1, lo, hi, base, r0, r1, c0, res, hyT = [ftile(n) for n in ("p1", "lo", "hi", "base", "r0", "r1", "c0", "res", "hyT")]
-        tt = nc.vector.tensor_tensor
-        stt = nc.vector.scalar_tensor_tensor
+        def turn(dst, src, block, scale):
+            ps = turn_bank()
+            nc.tensor.transpose(ps[:], src[:, cols(block)], ident[:])
+            nc.scalar.activation(dst[:, cols(block)], ps[:], COPY, scale=scale)
 
-        def turn_scaled(dst, src, first, n, col):
-            for i in range(first, first + n):
-                ps = psum.tile([P, BLK], F32, name="turn_ps", tag="turn", bufs=6)
-                nc.tensor.transpose(ps[:], src[:, cols(i, 1)], ident[:])
-                nc.scalar.activation(dst[:, cols(i, 1)], ps[:], COPY, scale=(0.5 if col is None else wcol[:, col + i : col + i + 1]))
+        def weight(table, d, block):
+            c = TURNED * d + block
+            return table[:, c : c + 1]
 
         def add_back(ps, src, first, n, start, stop):
             for i in range(n):
-                nc.tensor.matmul(ps[:, cols(i, 1)], src[:, cols(first + i, 1)], ident[:], start=(start and i == 0), stop=(stop and i == n - 1), is_transpose=True)
+                nc.tensor.matmul(ps[:, cols(i)], src[:, cols(first + i)], ident[:], start=(start and i == 0), stop=(stop and i == n - 1), is_transpose=True)
 
-        A, B = cols(0, 2), cols(2, 2)
-        c2, c3 = cols(2, 1), cols(3, 1)
-        turned = ((0, 2), (2, 1))
-        for j, (first, n) in enumerate(turned):
-            turn_scaled(hyT, y, first, n, None)
-        for j, (first, n) in enumerate(turned):
+        tt = nc.vector.tensor_tensor
+        stt = nc.vector.scalar_tensor_tensor
+        last = cols(LAST)
+        parts = ((0, 2), (2, 1))
+
+        g_pair = [field("g0"), field("g1")]
+        half_y_turned = field("half_y_turned", TURNED * BLK)
+        fwd_turned = [field("fwd_turned%d" % d, TURNED * BLK) for d in range(2)]
+        p1 = field("p1")
+        for block in range(TURNED):
+            turn(half_y_turned, y, block, 0.5)
+        for j, (first, n) in enumerate(parts):
             for d in range(2):
-                nc.vector.tensor_copy(g[d][:, cols(first, n)], y[:].indirect(entries(f[d], first, n)))
-                turn_scaled(tT[d], g[d], first, n, 4 * d)
-            p1_ps = psum.tile([P, n * BLK], F32, name="p1_ps%d" % j, tag="sum%d" % j)
+                gather(g_pair[d], y, fwd[d], first, n)
+                for block in range(first, first + n):
+                    turn(fwd_turned[d], g_pair[d], block, weight(wf_cols, d, block))
+            p1_ps = sum_bank(j, n, "p1_ps%d" % j)
             for d in range(2):
-                add_back(p1_ps, tT[d], first, n, d == 0, d == 1)
+                add_back(p1_ps, fwd_turned[d], first, n, d == 0, d == 1)
             nc.scalar.copy(p1[:, cols(first, n)], p1_ps[:])
+        fwd_last = [field("fwd_last%d" % d, BLK) for d in range(2)]
+        lo, hi = field("lo"), field("hi")
         for d in range(2):
-            nc.vector.tensor_copy(g[d][:, c3], y[:].indirect(entries(f[d], 3, 1)))
+            gather(g_pair[d], y, fwd[d], LAST, 1)
         for d in range(2):
-            tt(t[d][:, c3], g[d][:, c3], wf_t[:, d, :], ALU.mult)
-        tt(lo[:], g[0][:], g[1][:], ALU.min)
-        tt(p1[:, c3], t[0][:, c3], t[1][:, c3], ALU.add)
-        tt(hi[:], g[0][:], g[1][:], ALU.max)
-        rr = [psum.tile([P, n * BLK], F32, name="rr%d" % j, tag="sum%d" % j) for j, (first, n) in enumerate(turned)]
-        for j, (first, n) in enumerate(turned):
-            add_back(rr[j], hyT, first, n, True, False)
-            for d in range(2):
-                add_back(rr[j], tT[d], first, n, False, False)
+            tt(fwd_last[d][:], g_pair[d][:, last], wf_last[:, d, :], ALU.mult)
+        tt(lo[:], g_pair[0][:], g_pair[1][:], ALU.min)
+        tt(p1[:, last], fwd_last[0][:], fwd_last[1][:], ALU.add)
+        tt(hi[:], g_pair[0][:], g_pair[1][:], ALU.max)
 
-        for j, (first, n) in enumerate(turned):
+        rr_ps = [sum_bank(j, n, "rr_ps%d" % j) for j, (first, n) in enumerate(parts)]
+        for j, (first, n) in enumerate(parts):
+            add_back(rr_ps[j], half_y_turned, first, n, True, False)
             for d in range(2):
-                nc.vector.tensor_copy(u[d][:, cols(first, n)], p1[:].indirect(entries(b[d], first, n)))
-                turn_scaled(uT[d], u[d], first, n, 8 + 4 * d)
+                add_back(rr_ps[j], fwd_turned[d], first, n, False, False)
+        q_pair = [field("q%d" % d, TURNED * BLK) for d in range(2)]
+        bwd_turned = [field("bwd_turned%d" % d, TURNED * BLK) for d in range(2)]
+        for j, (first, n) in enumerate(parts):
             for d in range(2):
-                add_back(rr[j], uT[d], first, n, False, d == 1)
+                gather(q_pair[d], p1, bwd[d], first, n)
+                for block in range(first, first + n):
+                    turn(bwd_turned[d], q_pair[d], block, weight(wb_cols, d, block))
+            for d in range(2):
+                add_back(rr_ps[j], bwd_turned[d], first, n, False, d == 1)
+        bwd_last = [field("bwd_last%d" % d, BLK) for d in range(2)]
+        rr_last = [field("rr_last%d" % i, BLK) for i in range(3)]
         for d in range(2):
-            tt(u[d][:, c3], p1[:].indirect(entries(b[d], 3, 1)), wb_t[:, d, :], ALU.mult)
-        stt(base[:, c3], y[:, c3], 0.5, p1[:, c3], ALU.mult, ALU.add)
-        stt(r0[:, c3], u[0][:, c3], -0.5, base[:, c3], ALU.mult, ALU.add)
-        stt(r1[:, c3], u[1][:, c3], -0.5, r0[:, c3], ALU.mult, ALU.add)
-        tt(c0[:, c3], r1[:, c3], lo[:, c3], ALU.max)
-        tt(c0[:, A], rr[0][:], lo[:, A], ALU.max)
-        tt(c0[:, c2], rr[1][:], lo[:, c2], ALU.max)
-        tt(res[:, A], c0[:, A], hi[:, A], ALU.min)
-        nc.sync.dma_start(out[:, A], res[:, A])
-        tt(res[:, B], c0[:, B], hi[:, B], ALU.min)
-        nc.sync.dma_start(out[:, B], res[:, B])
+            tt(bwd_last[d][:], p1[:].indirect(entries(bwd[d], LAST, 1)), wb_last[:, d, :], ALU.mult)
+        stt(rr_last[0][:], y[:, last], 0.5, p1[:, last], ALU.mult, ALU.add)
+        for d in range(2):
+            stt(rr_last[d + 1][:], bwd_last[d][:], -0.5, rr_last[d][:], ALU.mult, ALU.add)
+
+        raised, result = field("raised"), field("result")
+        tt(raised[:, last], rr_last[2][:], lo[:, last], ALU.max)
+        for j, (first, n) in enumerate(parts):
+            tt(raised[:, cols(first, n)], rr_ps[j][:], lo[:, cols(first, n)], ALU.max)
+        for h in range(2):
+            c = cols(2 * h, 2)
+            tt(result[:, c], raised[:, c], hi[:, c], ALU.min)
+            nc.sync.dma_start(out[:, c], result[:, c])

@@ -169,12 +169,15 @@ def tile_picked_ymaccor_clamp_p_kernel(tc, x_words, x_scales, w1, wf, wb, offs, 
                 add_back(p1_ps, fwd_turned[d], first, n, d == 0, d == 1)
             nc.scalar.copy(p1[:, cols(first, n)], p1_ps[:])
         fwd_last = [field("fwd_last%d" % d, BLK) for d in range(2)]
-        lo, hi = field("lo"), field("hi")
+        raised = field("raised", S + BLK)
+        lo = [raised[:, cols(LAST, 2)], field("lo1", 2 * BLK)[:]]
+        hi = field("hi")
         for d in range(2):
             gather(g_pair[d], y, fwd[d], LAST, 1)
         for d in range(2):
             tt(fwd_last[d][:], g_pair[d][:, last], wf_last[:, d, :], ALU.mult)
-        tt(lo[:], g_pair[0][:], g_pair[1][:], ALU.min)
+        for h in range(2):
+            tt(lo[h], g_pair[0][:, cols(2 * h, 2)], g_pair[1][:, cols(2 * h, 2)], ALU.min)
         tt(p1[:, last], fwd_last[0][:], fwd_last[1][:], ALU.add)
         tt(hi[:], g_pair[0][:], g_pair[1][:], ALU.max)
 
@@ -200,10 +203,10 @@ def tile_picked_ymaccor_clamp_p_kernel(tc, x_words, x_scales, w1, wf, wb, offs, 
         for d in range(2):
             stt(rr_last[d + 1][:], bwd_last[d][:], -0.5, rr_last[d][:], ALU.mult, ALU.add)
 
-        raised, result = field("raised"), field("result")
-        tt(raised[:, last], rr_last[2][:], lo[:, last], ALU.max)
-        for j, (first, n) in enumerate(parts):
-            tt(raised[:, cols(first, n)], rr_ps[j][:], lo[:, cols(first, n)], ALU.max)
+        result = field("result")
+        tt(raised[:, cols(0, 2)], rr_ps[0][:], lo[0], ALU.max)
+        tt(raised[:, last], rr_last[2][:], lo[1][:, cols(1)], ALU.max)
+        tt(raised[:, cols(2)], rr_ps[1][:], lo[1][:, cols(0)], ALU.max)
         for h in range(2):
             c = cols(2 * h, 2)
             tt(result[:, c], raised[:, c], hi[:, c], ALU.min)

from contextlib import ExitStack

import concourse.mybir as mybir
from concourse.masks import make_identity

K, T, S, M = 1024, 2048, 512, 128
FLOPS = 2 * K * S * M

F32 = mybir.dt.float32
BF16 = mybir.dt.bfloat16
I32 = mybir.dt.int32
U32 = mybir.dt.uint32
U16 = mybir.dt.uint16
U8 = mybir.dt.uint8
FP8X4 = mybir.dt.float8_e4m3fn_x4
ALU = mybir.AluOpType
COPY = mybir.ActivationFunctionType.Copy

P = 128
PACK = 4
PASSES = K // (P * PACK)
QUADRANTS = P // 32
BLK = 128
BLOCKS = S // BLK
TURNED = BLOCKS - 1
LAST = TURNED
SUM_BANKS = 2
TURN_BANKS = 8 - SUM_BANKS


def tile_picked_ymaccor_clamp_p_kernel(tc, x_words, x_scales, w1, wf, wb, offs, fwd1, bwd1, fwd2, bwd2, out):
    nc = tc.nc
    with ExitStack() as ctx:
        lists = ctx.enter_context(tc.tile_pool(name="lists", bufs=1))
        sb = ctx.enter_context(tc.tile_pool(name="sb", bufs=1))
        psum = ctx.enter_context(tc.psum_pool(name="psum", bufs=1))

        def cols(first, n=1):
            return slice(first * BLK, (first + n) * BLK)

        def entries(lst, first, n):
            return lst[:, first * BLK // 16 : (first + n) * BLK // 16]

        def load_list(src, name):
            lst = lists.tile([P, S // 16], U16, name=name)
            nc.sync.dma_start(lst[:], src)
            return lst

        def field(name, width=S):
            return sb.tile([P, width], F32, name=name)

        def sum_bank(bank, n, name):
            return psum.tile([P, n * BLK], F32, name=name, tag="sum%d" % bank)

        def turn_bank():
            return psum.tile([P, BLK], F32, name="turn", tag="turn", bufs=TURN_BANKS)

        x_scale_table = sb.tile([P, T], U8, name="x_scale_table", align_bytes=64)
        nc.gpsimd.memset(x_scale_table[:].bitcast(I32), 0)
        weight_rows = field("weight_rows", BLK)
        nc.gpsimd.memset(weight_rows[:], 0.0)
        ident = field("ident", P)
        make_identity(nc, ident[:])

        x_word_table = [sb.tile([P, T], U32, name="x_word_table%d" % g, align_bytes=64) for g in range(PASSES)]
        w_raw = sb.tile([P, PASSES, PACK, M], F32, name="w_raw")

        def load_words(g):
            nc.sync.dma_start(x_word_table[g][:].bitcast(I32), x_words[g].rearrange("p n t -> p (n t)").bitcast(I32))

        def load_scales(q):
            for g in range(PASSES):
                row = 32 * q + 4 * g
                nc.sync.dma_start(x_scale_table[row : row + 4, :].bitcast(I32), x_scales[g, 4 * q : 4 * q + 4, :].bitcast(I32))

        idx = load_list(offs, "idx")
        nc.sync.dma_start(w_raw[:], w1.rearrange("(g p t) m -> p g t m", g=PASSES, t=PACK))
        load_scales(0)
        load_words(0)
        for q in range(1, QUADRANTS):
            load_scales(q)
        load_words(1)
        for s, weights in enumerate((wf, wb)):
            rows = weight_rows[2 * TURNED * s : 2 * TURNED * (s + 1), :]
            nc.gpsimd.dma_start(rows, weights[:, 0, cols(0, TURNED)].rearrange("d (b c) -> d b c", c=BLK))
        fwd = [load_list(fwd1, "f0"), load_list(fwd2, "f1")]
        wf_last = sb.tile([P, 2, BLK], F32, name="wf_last")
        nc.sync.dma_start(wf_last[:], wf[:, :, cols(LAST)].rearrange("d p c -> p d c"))
        bwd = [load_list(bwd1, "b0"), load_list(bwd2, "b1")]
        wb_last = sb.tile([P, 2, BLK], F32, name="wb_last")
        nc.sync.dma_start(wb_last[:], wb[:, :, cols(LAST)].rearrange("d p c -> p d c"))

        w_bf = sb.tile([P, PASSES, M, PACK], BF16, name="w_bf", align_bytes=64)
        nc.scalar.copy(w_bf[:], w_raw[:].rearrange("p g t m -> p g m t"))
        w_codes = sb.tile([P, PASSES * M], U32, name="w_codes", align_bytes=64)
        w_scales = sb.tile([P, PASSES * M], U8, name="w_scales", align_bytes=64)
        nc.vector.quantize_mx(out=w_codes[:].bitcast(FP8X4), scales=w_scales[:], in_=w_bf[:].rearrange("p g m t -> p (g m t)"))

        x_codes = [sb.tile([P, S], U32, name="x_codes%d" % g, align_bytes=64) for g in range(PASSES)]
        x_scale = sb.tile([P, S], U8, name="x_scale", align_bytes=64)
        nc.vector.tensor_copy(x_codes[0][:], x_word_table[0][:].indirect(idx[:]))
        nc.vector.tensor_copy(x_scale[:], x_scale_table[:].indirect(idx[:]))

        y_ps = [sum_bank(h, 2, "y_ps%d" % h) for h in range(2)]

        def product(h, g):
            c = cols(2 * h, 2)
            nc.tensor.matmul_mx(
                out=y_ps[h][:],
                lhsT=w_codes[:, g * M : (g + 1) * M].bitcast(FP8X4),
                lhsT_scale=w_scales[:, g * M : (g + 1) * M],
                rhs=x_codes[g][:, c].bitcast(FP8X4),
                rhs_scale=x_scale[4 * g : P, c],
                start=(g == 0),
                stop=(g == PASSES - 1),
            )

        for h in range(2):
            product(h, 0)

        weight_ps = turn_bank()
        nc.tensor.transpose(weight_ps[:], weight_rows[:], ident[:])
        wf_cols = field("wf_cols", 2 * TURNED)
        wb_cols = field("wb_cols", 2 * TURNED)
        nc.scalar.copy(wf_cols[:], weight_ps[:, 0 : 2 * TURNED])
        nc.scalar.activation(wb_cols[:], weight_ps[:, 2 * TURNED : 4 * TURNED], COPY, scale=-0.5)

        for h in range(2):
            nc.vector.tensor_copy(x_codes[1][:, cols(2 * h, 2)], x_word_table[1][:].indirect(entries(idx, 2 * h, 2)))
            product(h, 1)
        y = field("y")
        nc.scalar.copy(y[:, cols(0, 2)], y_ps[0][:])
        nc.vector.tensor_copy(y[:, cols(2, 2)], y_ps[1][:])

        def gather(dst, window, lst, first, n):
            nc.vector.tensor_copy(dst[:, cols(first, n)], window[:].indirect(entries(lst, first, n)))

        def turn(dst, src, block, scale):
            ps = turn_bank()
            nc.tensor.transpose(ps[:], src[:, cols(block)], ident[:])
            nc.scalar.activation(dst[:, cols(block)], ps[:], COPY, scale=scale)

        def weight(table, d, block):
            c = TURNED * d + block
            return table[:, c : c + 1]

        def add_back(ps, src, first, n, start, stop):
            for i in range(n):
                nc.tensor.matmul(ps[:, cols(i)], src[:, cols(first + i)], ident[:], start=(start and i == 0), stop=(stop and i == n - 1), is_transpose=True)

        tt = nc.vector.tensor_tensor
        stt = nc.vector.scalar_tensor_tensor
        last = cols(LAST)
        parts = ((0, 2), (2, 1))

        g_pair = [field("g0"), field("g1")]
        half_y_turned = field("half_y_turned", TURNED * BLK)
        fwd_turned = [field("fwd_turned%d" % d, TURNED * BLK) for d in range(2)]
        p1 = field("p1")
        for block in range(TURNED):
            turn(half_y_turned, y, block, 0.5)
        for j, (first, n) in enumerate(parts):
            for d in range(2):
                gather(g_pair[d], y, fwd[d], first, n)
                for block in range(first, first + n):
                    turn(fwd_turned[d], g_pair[d], block, weight(wf_cols, d, block))
            p1_ps = sum_bank(j, n, "p1_ps%d" % j)
            for d in range(2):
                add_back(p1_ps, fwd_turned[d], first, n, d == 0, d == 1)
            nc.scalar.copy(p1[:, cols(first, n)], p1_ps[:])
        fwd_last = [field("fwd_last%d" % d, BLK) for d in range(2)]
        raised = field("raised", S + BLK)
        lo = [raised[:, cols(LAST, 2)], field("lo1", 2 * BLK)[:]]
        hi = field("hi")
        for d in range(2):
            gather(g_pair[d], y, fwd[d], LAST, 1)
        for d in range(2):
            tt(fwd_last[d][:], g_pair[d][:, last], wf_last[:, d, :], ALU.mult)
        for h in range(2):
            tt(lo[h], g_pair[0][:, cols(2 * h, 2)], g_pair[1][:, cols(2 * h, 2)], ALU.min)
        tt(p1[:, last], fwd_last[0][:], fwd_last[1][:], ALU.add)
        tt(hi[:], g_pair[0][:], g_pair[1][:], ALU.max)

        rr_ps = [sum_bank(j, n, "rr_ps%d" % j) for j, (first, n) in enumerate(parts)]
        for j, (first, n) in enumerate(parts):
            add_back(rr_ps[j], half_y_turned, first, n, True, False)
            for d in range(2):
                add_back(rr_ps[j], fwd_turned[d], first, n, False, False)
        q_pair = [field("q%d" % d, TURNED * BLK) for d in range(2)]
        bwd_turned = [field("bwd_turned%d" % d, TURNED * BLK) for d in range(2)]
        for j, (first, n) in enumerate(parts):
            for d in range(2):
                gather(q_pair[d], p1, bwd[d], first, n)
                for block in range(first, first + n):
                    turn(bwd_turned[d], q_pair[d], block, weight(wb_cols, d, block))
            for d in range(2):
                add_back(rr_ps[j], bwd_turned[d], first, n, False, d == 1)
        bwd_last = [field("bwd_last%d" % d, BLK) for d in range(2)]
        rr_last = [field("rr_last%d" % i, BLK) for i in range(3)]
        for d in range(2):
            tt(bwd_last[d][:], p1[:].indirect(entries(bwd[d], LAST, 1)), wb_last[:, d, :], ALU.mult)
        stt(rr_last[0][:], y[:, last], 0.5, p1[:, last], ALU.mult, ALU.add)
        for d in range(2):
            stt(rr_last[d + 1][:], bwd_last[d][:], -0.5, rr_last[d][:], ALU.mult, ALU.add)

        result = field("result")
        tt(raised[:, cols(0, 2)], rr_ps[0][:], lo[0], ALU.max)
        tt(raised[:, last], rr_last[2][:], lo[1][:, cols(1)], ALU.max)
        tt(raised[:, cols(2)], rr_ps[1][:], lo[1][:, cols(0)], ALU.max)
        for h in range(2):
            c = cols(2 * h, 2)
            tt(result[:, c], raised[:, c], hi[:, c], ALU.min)
            nc.sync.dma_start(out[:, c], result[:, c])
